import numpy as np
import ml_dtypes


def mxq(x, axis, fmt="e4m3"):
    dtype, down = {"e4m3": (ml_dtypes.float8_e4m3fn, 7), "e5m2": (ml_dtypes.float8_e5m2, 14)}[fmt]
    v = np.moveaxis(np.asarray(x, np.float32).astype(ml_dtypes.bfloat16).astype(np.float64), axis, -1)
    blocks = v.reshape(v.shape[:-1] + (-1, 32))
    amax = np.abs(blocks).max(-1, keepdims=True)
    byte = np.maximum(np.where(amax > 0, np.frexp(amax)[1] - 1 + 127, 0) - down, 1)
    scale = np.exp2(byte - 127.0)
    codes = (blocks / scale).astype(np.float32).astype(dtype).astype(np.float64)
    return np.moveaxis((codes * scale).reshape(v.shape), -1, axis)


WIDE = False


def mx_kscale(k):
    if not WIDE:
        return np.ones(k)
    levels = np.array([10, -10, 5, -5, 0])
    if k % 512:
        return np.exp2(np.random.permutation(np.resize(levels, k // 32))).repeat(32)
    a = np.empty((k // 512, 16))
    for p in range(k // 512):
        a[p, :8] = np.random.permutation(np.resize(levels, 8))
        for g in range(8):
            far = levels[np.abs(levels - a[p, g]) >= 10]
            a[p, g + 8] = far[np.random.randint(len(far))]
    return np.exp2(a.ravel()).repeat(32)


def f64(x):
    return np.asarray(x).astype(np.float64)


def striped(idx):
    return np.tile(idx.reshape(-1, 16).T, (8, 1)).astype(np.uint16)


def unstriped(offs):
    return offs[:16].T.reshape(-1).astype(np.int64)


K, T, D, S, V, N = 512, 512, 6, 1536, 256, 256


def setup_inputs():
    n = np.random.standard_normal
    s = mx_kscale(K)[:, None]
    return {
        "xT": (n((K, T)) * s).astype(np.float32),
        "w": (n((K, N)) / np.sqrt(K) / s).astype(np.float32),
        "gate": np.tile(np.random.uniform(0.2, 1.0, (D, 1, V)) / np.sqrt(D), (1, N, 1)).astype(np.float32),
        "pos1": striped(np.random.permutation(T)[:V]),
        "pos2": striped(np.random.permutation(T)[:V]),
        "pos3": striped(np.random.permutation(T)[:V]),
        "pos4": striped(np.random.permutation(T)[:V]),
        "pos5": striped(np.random.permutation(T)[:V]),
        "pos6": striped(np.random.permutation(T)[:V]),
    }


def reference(xT, w, gate, pos1, pos2, pos3, pos4, pos5, pos6):
    y = mxq(f64(w), 0, "e4m3").T @ mxq(f64(xT), 0, "e4m3")
    return sum(f64(gate[d]) * y[:, unstriped(p)] for d, p in enumerate((pos1, pos2, pos3, pos4, pos5, pos6)))

@@ -1,0 +1,174 @@
+from contextlib import ExitStack
+
+import concourse.mybir as mybir
+from concourse.masks import make_identity
+
+K, T, D, V, N = 512, 512, 6, 256, 256
+FLOPS = 2 * K * T * N
+
+F32 = mybir.dt.float32
+BF16 = mybir.dt.bfloat16
+U32 = mybir.dt.uint32
+U16 = mybir.dt.uint16
+U8 = mybir.dt.uint8
+FP8X4 = mybir.dt.float8_e4m3fn_x4
+MULT = mybir.AluOpType.mult
+
+P = 128
+PACK = 4
+TA = 256
+B1 = 128
+B2_SCALAR = 88
+BY_TENSOR = 4
+
+
+def interleave(cast, dst, src):
+    cast(
+        dst.rearrange("p (c i) j -> p c j i", i=4),
+        src.rearrange("p j (c i) -> p c j i", i=4),
+    )
+
+
+def tile_picked_agg_lin_none_sub_l_kernel(
+    tc, xT, w, gate, pos1, pos2, pos3, pos4, pos5, pos6, out
+):
+    nc = tc.nc
+    lists = (pos1, pos2, pos3, pos4, pos5, pos6)
+    x_rows = xT.rearrange("(p j) t -> p j t", j=PACK)
+    w_rows = w.rearrange("(p j) m -> p j m", j=PACK)
+
+    def vcopy(dst, src):
+        nc.vector.tensor_copy(dst, src)
+
+    def scopy(dst, src):
+        nc.scalar.copy(dst, src)
+
+    with ExitStack() as ctx:
+        keep = ctx.enter_context(tc.tile_pool(name="keep", bufs=1))
+        ring = ctx.enter_context(tc.tile_pool(name="ring", bufs=4))
+        psum = ctx.enter_context(tc.psum_pool(name="psum", bufs=1))
+
+        offs = [keep.tile([P, V // 16], U16, name=f"offs{d}") for d in range(D)]
+        ident = keep.tile([P, P], F32, name="ident")
+        make_identity(nc, ident[:])
+
+        w_raw = [keep.tile([P, PACK, P], F32, name=f"w_raw{h}") for h in range(2)]
+        xa_raw = keep.tile([P, PACK, TA], F32, name="xa_raw")
+        xb_raw = keep.tile([P, PACK, T - TA], F32, name="xb_raw")
+        gates = [[keep.tile([P, 3, V], F32, name=f"gate{h}{q}") for q in range(2)] for h in range(2)]
+
+        def load_gate(h, q):
+            nc.sync.dma_start(
+                gates[h][q][:],
+                gate[3 * q : 3 * q + 3, P * h : P * h + P, :].rearrange("d p v -> p d v"),
+            )
+
+        nc.sync.dma_start(w_raw[0][:], w_rows[:, :, 0:P])
+        nc.sync.dma_start(xa_raw[:], x_rows[:, :, 0:TA])
+        nc.sync.dma_start(xb_raw[:], x_rows[:, :, TA:T])
+        nc.sync.dma_start(offs[0][:], lists[0])
+        nc.sync.dma_start(offs[1][:], lists[1])
+        load_gate(0, 0)
+        nc.sync.dma_start(w_raw[1][:], w_rows[:, :, P : 2 * P])
+        for d in range(2, D):
+            nc.sync.dma_start(offs[d][:], lists[d])
+        load_gate(0, 1)
+        load_gate(1, 0)
+        load_gate(1, 1)
+
+        x_codes = keep.tile([P, T], U32, name="x_codes", align_bytes=64)
+        x_scales = keep.tile([P, T], U8, name="x_scales", align_bytes=64)
+        w_codes = [keep.tile([P, P], U32, name=f"w_codes{h}", align_bytes=64) for h in range(2)]
+        w_scales = [keep.tile([P, P], U8, name=f"w_scales{h}", align_bytes=64) for h in range(2)]
+        w_bf = [keep.tile([P, P, PACK], BF16, name=f"w_bf{h}", align_bytes=64) for h in range(2)]
+        xa_bf = keep.tile([P, TA, PACK], BF16, name="xa_bf", align_bytes=64)
+        xb1_bf = keep.tile([P, B1, PACK], BF16, name="xb1_bf", align_bytes=64)
+        xb2_bf = keep.tile([P, T - TA - B1, PACK], BF16, name="xb2_bf", align_bytes=64)
+
+        def quantise(codes, scales, src):
+            nc.vector.quantize_mx(
+                out=codes.bitcast(FP8X4), scales=scales, in_=src[:].rearrange("p c j -> p (c j)")
+            )
+
+        def multiply(dst, h, t0, t1):
+            nc.tensor.matmul_mx(
+                out=dst,
+                lhsT=w_codes[h][:].bitcast(FP8X4),
+                lhsT_scale=w_scales[h][:],
+                rhs=x_codes[:, t0:t1].bitcast(FP8X4),
+                rhs_scale=x_scales[:, t0:t1],
+                start=True,
+                stop=True,
+            )
+
+        y = [keep.tile([P, T], F32, name=f"y{h}") for h in range(2)]
+        ya_ps = psum.tile([P, TA], F32, name="ya_ps")
+        yb1_ps = psum.tile([P, B1], F32, name="yb1_ps")
+        yb2_ps = psum.tile([P, T - TA - B1], F32, name="yb2_ps")
+        y1_ps = psum.tile([P, T], F32, name="y1_ps")
+
+        interleave(vcopy, w_bf[0][:], w_raw[0][:])
+        interleave(scopy, xa_bf[:, 0 : TA // 2, :], xa_raw[:, :, 0 : TA // 2])
+        interleave(vcopy, xa_bf[:, TA // 2 : TA, :], xa_raw[:, :, TA // 2 : TA])
+        quantise(w_codes[0][:], w_scales[0][:], w_bf[0])
+        quantise(x_codes[:, 0:TA], x_scales[:, 0:TA], xa_bf)
+        multiply(ya_ps[:], 0, 0, TA)
+        nc.scalar.copy(y[0][:, 0:TA], ya_ps[:])
+
+        interleave(scopy, xb2_bf[:, 0:B2_SCALAR, :], xb_raw[:, :, B1 : B1 + B2_SCALAR])
+        interleave(vcopy, xb1_bf[:], xb_raw[:, :, 0:B1])
+        interleave(vcopy, xb2_bf[:, B2_SCALAR:, :], xb_raw[:, :, B1 + B2_SCALAR :])
+        quantise(x_codes[:, TA : TA + B1], x_scales[:, TA : TA + B1], xb1_bf)
+        quantise(x_codes[:, TA + B1 : T], x_scales[:, TA + B1 : T], xb2_bf)
+        multiply(yb1_ps[:], 0, TA, TA + B1)
+        multiply(yb2_ps[:], 0, TA + B1, T)
+        nc.scalar.copy(y[0][:, TA : TA + B1], yb1_ps[:])
+        nc.vector.tensor_copy(y[0][:, TA + B1 : T], yb2_ps[:])
+
+        def gather(h, d):
+            g = ring.tile([P, V], F32, name="g")
+            nc.vector.tensor_tensor(
+                g[:], y[h][:].indirect(offs[d][:]), gates[h][d // 3][:, d % 3, :], MULT
+            )
+            return g
+
+        def turn(dst, src, first, last):
+            nc.tensor.matmul(dst, src, ident[:], start=first, stop=last, is_transpose=True)
+
+        def tensor_sum(h, count, before):
+            acc = [psum.tile([P, P], F32, name=f"acc{b}") for b in range(2)]
+            for d in range(count):
+                g = gather(h, d)
+                before(d)
+                for b in range(2):
+                    turn(acc[b][:], g[:, P * b : P * b + P], d == 0, d == count - 1)
+            turned = ring.tile([P, 2, P], F32, name="turned")
+            back = psum.tile([P, V], F32, name="back")
+            for b in range(2):
+                nc.scalar.copy(turned[:, b, :], acc[b][:])
+            for b in range(2):
+                turn(back[:, P * b : P * b + P], turned[:, b, :], True, True)
+            return back
+
+        def second_half(d):
+            if d == 1:
+                interleave(scopy, w_bf[1][:], w_raw[1][:])
+                quantise(w_codes[1][:], w_scales[1][:], w_bf[1])
+                multiply(y1_ps[:], 1, 0, T)
+                nc.scalar.copy(y[1][:], y1_ps[:])
+
+        back = tensor_sum(0, D, second_half)
+        result = ring.tile([P, V], F32, name="result")
+        nc.scalar.copy(result[:], back[:])
+        nc.sync.dma_start(out[0:P, :], result[:])
+
+        back = tensor_sum(1, BY_TENSOR, lambda d: None)
+        g4 = gather(1, 4)
+        g5 = gather(1, 5)
+        late = ring.tile([P, V], F32, name="late")
+        nc.vector.tensor_add(late[:], g4[:], g5[:])
+        result = ring.tile([P, V], F32, name="result")
+        for b in range(2):
+            cols = slice(P * b, P * b + P)
+            nc.vector.tensor_add(result[:, cols], late[:, cols], back[:, cols])
+            nc.sync.dma_start(out[P : 2 * P, cols], result[:, cols])

@@ -16,9 +16,8 @@ MULT = mybir.AluOpType.mult
 
 P = 128
 PACK = 4
-TA = 256
-B1 = 128
-B2_SCALAR = 88
+CHUNKS = ((0, 256), (256, 384), (384, 512))
+ON_SCALAR = (96, 48, 48)
 BY_TENSOR = 4
 
 
@@ -53,37 +52,40 @@ def tile_picked_agg_lin_none_sub_l_kernel(
         make_identity(nc, ident[:])
 
         w_raw = [keep.tile([P, PACK, P], F32, name=f"w_raw{h}") for h in range(2)]
-        xa_raw = keep.tile([P, PACK, TA], F32, name="xa_raw")
-        xb_raw = keep.tile([P, PACK, T - TA], F32, name="xb_raw")
-        gates = [[keep.tile([P, 3, V], F32, name=f"gate{h}{q}") for q in range(2)] for h in range(2)]
+        x_raw = [keep.tile([P, PACK, t1 - t0], F32, name=f"x_raw{t0}") for t0, t1 in CHUNKS]
+        gates = [keep.tile([P, D, V], F32, name=f"gates{h}") for h in range(2)]
 
-        def load_gate(h, q):
+        def load_gate(h, d0, d1):
             nc.sync.dma_start(
-                gates[h][q][:],
-                gate[3 * q : 3 * q + 3, P * h : P * h + P, :].rearrange("d p v -> p d v"),
+                gates[h][:, d0:d1, :], gate[d0:d1, P * h : P * h + P, :].rearrange("d p v -> p d v")
             )
 
-        nc.sync.dma_start(w_raw[0][:], w_rows[:, :, 0:P])
-        nc.sync.dma_start(xa_raw[:], x_rows[:, :, 0:TA])
-        nc.sync.dma_start(xb_raw[:], x_rows[:, :, TA:T])
-        nc.sync.dma_start(offs[0][:], lists[0])
-        nc.sync.dma_start(offs[1][:], lists[1])
-        load_gate(0, 0)
-        nc.sync.dma_start(w_raw[1][:], w_rows[:, :, P : 2 * P])
-        for d in range(2, D):
+        def load_list(d):
             nc.sync.dma_start(offs[d][:], lists[d])
-        load_gate(0, 1)
-        load_gate(1, 0)
-        load_gate(1, 1)
+
+        nc.sync.dma_start(w_raw[0][:], w_rows[:, :, 0:P])
+        for raw, (t0, t1) in zip(x_raw, CHUNKS):
+            nc.sync.dma_start(raw[:], x_rows[:, :, t0:t1])
+        load_list(0)
+        load_gate(0, 0, 1)
+        load_list(1)
+        load_gate(0, 1, 2)
+        nc.sync.dma_start(w_raw[1][:], w_rows[:, :, P : 2 * P])
+        load_list(2)
+        load_list(3)
+        load_gate(0, 2, 4)
+        load_list(4)
+        load_list(5)
+        load_gate(0, 4, 6)
+        load_gate(1, 0, 3)
+        load_gate(1, 3, 6)
 
         x_codes = keep.tile([P, T], U32, name="x_codes", align_bytes=64)
         x_scales = keep.tile([P, T], U8, name="x_scales", align_bytes=64)
         w_codes = [keep.tile([P, P], U32, name=f"w_codes{h}", align_bytes=64) for h in range(2)]
         w_scales = [keep.tile([P, P], U8, name=f"w_scales{h}", align_bytes=64) for h in range(2)]
         w_bf = [keep.tile([P, P, PACK], BF16, name=f"w_bf{h}", align_bytes=64) for h in range(2)]
-        xa_bf = keep.tile([P, TA, PACK], BF16, name="xa_bf", align_bytes=64)
-        xb1_bf = keep.tile([P, B1, PACK], BF16, name="xb1_bf", align_bytes=64)
-        xb2_bf = keep.tile([P, T - TA - B1, PACK], BF16, name="xb2_bf", align_bytes=64)
+        x_bf = [keep.tile([P, t1 - t0, PACK], BF16, name=f"x_bf{t0}", align_bytes=64) for t0, t1 in CHUNKS]
 
         def quantise(codes, scales, src):
             nc.vector.quantize_mx(
@@ -102,33 +104,24 @@ def tile_picked_agg_lin_none_sub_l_kernel(
             )
 
         y = [keep.tile([P, T], F32, name=f"y{h}") for h in range(2)]
-        ya_ps = psum.tile([P, TA], F32, name="ya_ps")
-        yb1_ps = psum.tile([P, B1], F32, name="yb1_ps")
-        yb2_ps = psum.tile([P, T - TA - B1], F32, name="yb2_ps")
+        y0_ps = [psum.tile([P, t1 - t0], F32, name=f"y0_ps{t0}") for t0, t1 in CHUNKS]
         y1_ps = psum.tile([P, T], F32, name="y1_ps")
 
         interleave(vcopy, w_bf[0][:], w_raw[0][:])
-        interleave(scopy, xa_bf[:, 0 : TA // 2, :], xa_raw[:, :, 0 : TA // 2])
-        interleave(vcopy, xa_bf[:, TA // 2 : TA, :], xa_raw[:, :, TA // 2 : TA])
         quantise(w_codes[0][:], w_scales[0][:], w_bf[0])
-        quantise(x_codes[:, 0:TA], x_scales[:, 0:TA], xa_bf)
-        multiply(ya_ps[:], 0, 0, TA)
-        nc.scalar.copy(y[0][:, 0:TA], ya_ps[:])
-
-        interleave(scopy, xb2_bf[:, 0:B2_SCALAR, :], xb_raw[:, :, B1 : B1 + B2_SCALAR])
-        interleave(vcopy, xb1_bf[:], xb_raw[:, :, 0:B1])
-        interleave(vcopy, xb2_bf[:, B2_SCALAR:, :], xb_raw[:, :, B1 + B2_SCALAR :])
-        quantise(x_codes[:, TA : TA + B1], x_scales[:, TA : TA + B1], xb1_bf)
-        quantise(x_codes[:, TA + B1 : T], x_scales[:, TA + B1 : T], xb2_bf)
-        multiply(yb1_ps[:], 0, TA, TA + B1)
-        multiply(yb2_ps[:], 0, TA + B1, T)
-        nc.scalar.copy(y[0][:, TA : TA + B1], yb1_ps[:])
-        nc.vector.tensor_copy(y[0][:, TA + B1 : T], yb2_ps[:])
+        for raw, bf, bank, cut, (t0, t1) in zip(x_raw, x_bf, y0_ps, ON_SCALAR, CHUNKS):
+            interleave(scopy, bf[:, 0:cut, :], raw[:, :, 0:cut])
+            interleave(vcopy, bf[:, cut:, :], raw[:, :, cut:])
+            quantise(x_codes[:, t0:t1], x_scales[:, t0:t1], bf)
+            multiply(bank[:], 0, t0, t1)
+        for c in range(3):
+            t0, t1 = CHUNKS[c]
+            (scopy, scopy, vcopy)[c](y[0][:, t0:t1], y0_ps[c][:])
 
         def gather(h, d):
             g = ring.tile([P, V], F32, name="g")
             nc.vector.tensor_tensor(
-                g[:], y[h][:].indirect(offs[d][:]), gates[h][d // 3][:, d % 3, :], MULT
+                g[:], y[h][:].indirect(offs[d][:]), gates[h][:, d, :], MULT
             )
             return g
 
@@ -164,11 +157,16 @@ def tile_picked_agg_lin_none_sub_l_kernel(
 
         back = tensor_sum(1, BY_TENSOR, lambda d: None)
         g4 = gather(1, 4)
-        g5 = gather(1, 5)
-        late = ring.tile([P, V], F32, name="late")
-        nc.vector.tensor_add(late[:], g4[:], g5[:])
         result = ring.tile([P, V], F32, name="result")
+        late = ring.tile([P, V], F32, name="late")
+        blocks = [slice(P * b, P * b + P) for b in range(2)]
+        g5 = [ring.tile([P, P], F32, name=f"g5{b}") for b in range(2)]
         for b in range(2):
-            cols = slice(P * b, P * b + P)
-            nc.vector.tensor_add(result[:, cols], late[:, cols], back[:, cols])
-            nc.sync.dma_start(out[P : 2 * P, cols], result[:, cols])
+            nc.vector.tensor_tensor(
+                g5[b][:], y[1][:].indirect(offs[5][:, 8 * b : 8 * b + 8]), gates[1][:, 5, blocks[b]], MULT
+            )
+        for b in range(2):
+            nc.vector.tensor_add(late[:, blocks[b]], g4[:, blocks[b]], g5[b][:])
+        for b in range(2):
+            nc.vector.tensor_add(result[:, blocks[b]], late[:, blocks[b]], back[:, blocks[b]])
+            nc.sync.dma_start(out[P : 2 * P, blocks[b]], result[:, blocks[b]])

@@ -116,7 +116,7 @@ def tile_picked_agg_lin_none_sub_l_kernel(
             multiply(bank[:], 0, t0, t1)
         for c in range(3):
             t0, t1 = CHUNKS[c]
-            (scopy, scopy, vcopy)[c](y[0][:, t0:t1], y0_ps[c][:])
+            (scopy, vcopy, scopy)[c](y[0][:, t0:t1], y0_ps[c][:])
 
         def gather(h, d):
             g = ring.tile([P, V], F32, name="g")
@@ -136,11 +136,10 @@ def tile_picked_agg_lin_none_sub_l_kernel(
                 for b in range(2):
                     turn(acc[b][:], g[:, P * b : P * b + P], d == 0, d == count - 1)
             turned = ring.tile([P, 2, P], F32, name="turned")
-            back = psum.tile([P, V], F32, name="back")
+            back = [psum.tile([P, P], F32, name=f"back{b}") for b in range(2)]
             for b in range(2):
                 nc.scalar.copy(turned[:, b, :], acc[b][:])
-            for b in range(2):
-                turn(back[:, P * b : P * b + P], turned[:, b, :], True, True)
+                turn(back[b][:], turned[:, b, :], True, True)
             return back
 
         def second_half(d):
@@ -152,7 +151,8 @@ def tile_picked_agg_lin_none_sub_l_kernel(
 
         back = tensor_sum(0, D, second_half)
         result = ring.tile([P, V], F32, name="result")
-        nc.scalar.copy(result[:], back[:])
+        for b in range(2):
+            nc.scalar.copy(result[:, P * b : P * b + P], back[b][:])
         nc.sync.dma_start(out[0:P, :], result[:])
 
         back = tensor_sum(1, BY_TENSOR, lambda d: None)
@@ -168,5 +168,5 @@ def tile_picked_agg_lin_none_sub_l_kernel(
         for b in range(2):
             nc.vector.tensor_add(late[:, blocks[b]], g4[:, blocks[b]], g5[b][:])
         for b in range(2):
-            nc.vector.tensor_add(result[:, blocks[b]], late[:, blocks[b]], back[:, blocks[b]])
+            nc.vector.tensor_add(result[:, blocks[b]], late[:, blocks[b]], back[b][:])
             nc.sync.dma_start(out[P : 2 * P, blocks[b]], result[:, blocks[b]])

from contextlib import ExitStack

import concourse.mybir as mybir
from concourse.masks import make_identity

K, T, D, V, N = 512, 512, 6, 256, 256
FLOPS = 2 * K * T * N

F32 = mybir.dt.float32
BF16 = mybir.dt.bfloat16
U32 = mybir.dt.uint32
U16 = mybir.dt.uint16
U8 = mybir.dt.uint8
FP8X4 = mybir.dt.float8_e4m3fn_x4
MULT = mybir.AluOpType.mult

P = 128
PACK = 4
CHUNKS = ((0, 256), (256, 384), (384, 512))
ON_SCALAR = (96, 48, 48)
BY_TENSOR = 4


def interleave(cast, dst, src):
    cast(
        dst.rearrange("p (c i) j -> p c j i", i=4),
        src.rearrange("p j (c i) -> p c j i", i=4),
    )


def tile_picked_agg_lin_none_sub_l_kernel(
    tc, xT, w, gate, pos1, pos2, pos3, pos4, pos5, pos6, out
):
    nc = tc.nc
    lists = (pos1, pos2, pos3, pos4, pos5, pos6)
    x_rows = xT.rearrange("(p j) t -> p j t", j=PACK)
    w_rows = w.rearrange("(p j) m -> p j m", j=PACK)

    def vcopy(dst, src):
        nc.vector.tensor_copy(dst, src)

    def scopy(dst, src):
        nc.scalar.copy(dst, src)

    with ExitStack() as ctx:
        keep = ctx.enter_context(tc.tile_pool(name="keep", bufs=1))
        ring = ctx.enter_context(tc.tile_pool(name="ring", bufs=4))
        psum = ctx.enter_context(tc.psum_pool(name="psum", bufs=1))

        offs = [keep.tile([P, V // 16], U16, name=f"offs{d}") for d in range(D)]
        ident = keep.tile([P, P], F32, name="ident")
        make_identity(nc, ident[:])

        w_raw = [keep.tile([P, PACK, P], F32, name=f"w_raw{h}") for h in range(2)]
        x_raw = [keep.tile([P, PACK, t1 - t0], F32, name=f"x_raw{t0}") for t0, t1 in CHUNKS]
        gates = [keep.tile([P, D, V], F32, name=f"gates{h}") for h in range(2)]

        def load_gate(h, d0, d1):
            nc.sync.dma_start(
                gates[h][:, d0:d1, :], gate[d0:d1, P * h : P * h + P, :].rearrange("d p v -> p d v")
            )

        def load_list(d):
            nc.sync.dma_start(offs[d][:], lists[d])

        nc.sync.dma_start(w_raw[0][:], w_rows[:, :, 0:P])
        for raw, (t0, t1) in zip(x_raw, CHUNKS):
            nc.sync.dma_start(raw[:], x_rows[:, :, t0:t1])
        load_list(0)
        load_gate(0, 0, 1)
        load_list(1)
        load_gate(0, 1, 2)
        nc.sync.dma_start(w_raw[1][:], w_rows[:, :, P : 2 * P])
        load_list(2)
        load_list(3)
        load_gate(0, 2, 4)
        load_list(4)
        load_list(5)
        load_gate(0, 4, 6)
        load_gate(1, 0, 3)
        load_gate(1, 3, 6)

        x_codes = keep.tile([P, T], U32, name="x_codes", align_bytes=64)
        x_scales = keep.tile([P, T], U8, name="x_scales", align_bytes=64)
        w_codes = [keep.tile([P, P], U32, name=f"w_codes{h}", align_bytes=64) for h in range(2)]
        w_scales = [keep.tile([P, P], U8, name=f"w_scales{h}", align_bytes=64) for h in range(2)]
        w_bf = [keep.tile([P, P, PACK], BF16, name=f"w_bf{h}", align_bytes=64) for h in range(2)]
        x_bf = [keep.tile([P, t1 - t0, PACK], BF16, name=f"x_bf{t0}", align_bytes=64) for t0, t1 in CHUNKS]

        def quantise(codes, scales, src):
            nc.vector.quantize_mx(
                out=codes.bitcast(FP8X4), scales=scales, in_=src[:].rearrange("p c j -> p (c j)")
            )

        def multiply(dst, h, t0, t1):
            nc.tensor.matmul_mx(
                out=dst,
                lhsT=w_codes[h][:].bitcast(FP8X4),
                lhsT_scale=w_scales[h][:],
                rhs=x_codes[:, t0:t1].bitcast(FP8X4),
                rhs_scale=x_scales[:, t0:t1],
                start=True,
                stop=True,
            )

        y = [keep.tile([P, T], F32, name=f"y{h}") for h in range(2)]
        y0_ps = [psum.tile([P, t1 - t0], F32, name=f"y0_ps{t0}") for t0, t1 in CHUNKS]
        y1_ps = psum.tile([P, T], F32, name="y1_ps")

        interleave(vcopy, w_bf[0][:], w_raw[0][:])
        quantise(w_codes[0][:], w_scales[0][:], w_bf[0])
        for raw, bf, bank, cut, (t0, t1) in zip(x_raw, x_bf, y0_ps, ON_SCALAR, CHUNKS):
            interleave(scopy, bf[:, 0:cut, :], raw[:, :, 0:cut])
            interleave(vcopy, bf[:, cut:, :], raw[:, :, cut:])
            quantise(x_codes[:, t0:t1], x_scales[:, t0:t1], bf)
            multiply(bank[:], 0, t0, t1)
        for c in range(3):
            t0, t1 = CHUNKS[c]
            (scopy, vcopy, scopy)[c](y[0][:, t0:t1], y0_ps[c][:])

        def gather(h, d):
            g = ring.tile([P, V], F32, name="g")
            nc.vector.tensor_tensor(
                g[:], y[h][:].indirect(offs[d][:]), gates[h][:, d, :], MULT
            )
            return g

        def turn(dst, src, first, last):
            nc.tensor.matmul(dst, src, ident[:], start=first, stop=last, is_transpose=True)

        def tensor_sum(h, count, before):
            acc = [psum.tile([P, P], F32, name=f"acc{b}") for b in range(2)]
            for d in range(count):
                g = gather(h, d)
                before(d)
                for b in range(2):
                    turn(acc[b][:], g[:, P * b : P * b + P], d == 0, d == count - 1)
            turned = ring.tile([P, 2, P], F32, name="turned")
            back = [psum.tile([P, P], F32, name=f"back{b}") for b in range(2)]
            for b in range(2):
                nc.scalar.copy(turned[:, b, :], acc[b][:])
                turn(back[b][:], turned[:, b, :], True, True)
            return back

        def second_half(d):
            if d == 1:
                interleave(scopy, w_bf[1][:], w_raw[1][:])
                quantise(w_codes[1][:], w_scales[1][:], w_bf[1])
                multiply(y1_ps[:], 1, 0, T)
                nc.scalar.copy(y[1][:], y1_ps[:])

        back = tensor_sum(0, D, second_half)
        result = ring.tile([P, V], F32, name="result")
        for b in range(2):
            nc.scalar.copy(result[:, P * b : P * b + P], back[b][:])
        nc.sync.dma_start(out[0:P, :], result[:])

        back = tensor_sum(1, BY_TENSOR, lambda d: None)
        g4 = gather(1, 4)
        result = ring.tile([P, V], F32, name="result")
        late = ring.tile([P, V], F32, name="late")
        blocks = [slice(P * b, P * b + P) for b in range(2)]
        g5 = [ring.tile([P, P], F32, name=f"g5{b}") for b in range(2)]
        for b in range(2):
            nc.vector.tensor_tensor(
                g5[b][:], y[1][:].indirect(offs[5][:, 8 * b : 8 * b + 8]), gates[1][:, 5, blocks[b]], MULT
            )
        for b in range(2):
            nc.vector.tensor_add(late[:, blocks[b]], g4[:, blocks[b]], g5[b][:])
        for b in range(2):
            nc.vector.tensor_add(result[:, blocks[b]], late[:, blocks[b]], back[b][:])
            nc.sync.dma_start(out[P : 2 * P, blocks[b]], result[:, blocks[b]])
